import numpy as np
import ml_dtypes


def mxq(x, axis, fmt="e4m3"):
    dtype, down = {"e4m3": (ml_dtypes.float8_e4m3fn, 7), "e5m2": (ml_dtypes.float8_e5m2, 14)}[fmt]
    v = np.moveaxis(np.asarray(x, np.float32).astype(ml_dtypes.bfloat16).astype(np.float64), axis, -1)
    blocks = v.reshape(v.shape[:-1] + (-1, 32))
    amax = np.abs(blocks).max(-1, keepdims=True)
    byte = np.maximum(np.where(amax > 0, np.frexp(amax)[1] - 1 + 127, 0) - down, 1)
    scale = np.exp2(byte - 127.0)
    codes = (blocks / scale).astype(np.float32).astype(dtype).astype(np.float64)
    return np.moveaxis((codes * scale).reshape(v.shape), -1, axis)


WIDE = False


def mx_kscale(k):
    if not WIDE:
        return np.ones(k)
    levels = np.array([18, -18])
    if k % 512:
        return np.exp2(np.random.permutation(np.resize(levels, k // 32))).repeat(32)
    a = np.empty((k // 512, 16))
    for p in range(k // 512):
        a[p, :8] = np.random.permutation(np.resize(levels, 8))
        for g in range(8):
            far = levels[np.abs(levels - a[p, g]) >= 10]
            a[p, g + 8] = far[np.random.randint(len(far))]
    return np.exp2(a.ravel()).repeat(32)


def f64(x):
    return np.asarray(x).astype(np.float64)


def striped(idx):
    return np.tile(np.asarray(idx).reshape(-1, 16).T, (8, 1)).astype(np.uint16)


def unstriped(offs):
    return offs[:16].T.reshape(-1).astype(np.int64)


E2M1 = np.array([0.0, 0.5, 1.0, 1.5, 2.0, 3.0, 4.0, 6.0, -0.0, -0.5, -1.0, -1.5, -2.0, -3.0, -4.0, -6.0])


def pack_weight(w, fmt):
    k, n = w.shape
    w = f64(np.asarray(w, np.float32).astype(ml_dtypes.bfloat16)).reshape(k // 32, 32, n)
    amax = np.abs(w).max(1)
    if fmt == "e4m3":
        byte = np.frexp(amax)[1] - 1 + 127 - 7
    else:
        mant, ex = np.frexp(amax / 6.0)
        byte = np.where(mant > 0.5, ex, ex - 1) + 127
    byte = np.clip(np.where(amax > 0, byte, 1), 1, 254)
    scaled = (w * np.exp2(127.0 - byte)[:, None, :]).reshape(k, n).astype(np.float32)
    by_word = np.ascontiguousarray(scaled.reshape(k // 512, 128, 4, n).transpose(0, 1, 3, 2))
    if fmt == "e4m3":
        words = by_word.astype(ml_dtypes.float8_e4m3fn).view(np.uint8)
    else:
        c = by_word.astype(ml_dtypes.float4_e2m1fn).view(np.uint8) & 0xF
        words = (c[..., 0::2] | (c[..., 1::2] << 4)).reshape(k // 512, 128, 2 * n)
    return np.ascontiguousarray(words), np.ascontiguousarray(byte.astype(np.uint8).reshape(k // 512, 16, n))


def unpack_weight(words, scales, fmt):
    g, _, n = scales.shape
    words = np.ascontiguousarray(words).reshape(g, 128, n, -1)
    if fmt == "e4m3":
        vals = words.view(ml_dtypes.float8_e4m3fn).astype(np.float64)
    else:
        nib = np.empty((g, 128, n, 4), np.uint8)
        nib[..., 0::2] = words & 0xF
        nib[..., 1::2] = words >> 4
        vals = E2M1[nib]
    vals = vals * np.repeat(np.exp2(scales.astype(np.float64) - 127.0), 8, axis=1)[..., None]
    return vals.transpose(0, 1, 3, 2).reshape(g * 512, n)


V, K, E, D, DV = 512, 2, 1024, 512, 1024


def setup_inputs():
    n = np.random.standard_normal
    v = mx_kscale(DV)[:, None]
    coarse = lambda x: x.astype(np.float32).astype(ml_dtypes.bfloat16).astype(np.float64)
    wp = pack_weight(n((DV, D)) / np.sqrt(DV) / v, "e4m3")
    return {
        "dyT": (coarse(n((DV, V))) * v).astype(np.float32),
        "hE": coarse(n((DV, E))).astype(np.float32),
        "ew": np.tile(np.random.randint(8, 33, E) / 16.0, (128, 1)).astype(np.float32),
        "w_words": wp[0],
        "w_scales": wp[1],
        "offs": striped(np.random.randint(0, V, E)),
        "offs2": striped(np.random.permutation(E)),
    }


def reference(dyT, hE, ew, w_words, w_scales, offs, offs2):
    h = f64(hE)
    dz = f64(ew)[:1] * f64(dyT)[:, unstriped(offs)] * 2.0 * np.maximum(h, 0.0)
    dm = unpack_weight(w_words, w_scales, "e4m3").T @ mxq(dz, 0, "e5m2")
    return dm[:, unstriped(offs2)].reshape(D, V, K).sum(-1)

@@ -1,0 +1,233 @@
+from contextlib import ExitStack
+
+import concourse.mybir as mybir
+from concourse.masks import make_identity
+
+V, K, E, D, DV = 512, 2, 1024, 512, 1024
+FLOPS = 2 * DV * D * E
+
+F32 = mybir.dt.float32
+BF16 = mybir.dt.bfloat16
+I32 = mybir.dt.int32
+U32 = mybir.dt.uint32
+U16 = mybir.dt.uint16
+U8 = mybir.dt.uint8
+E4M3X4 = mybir.dt.float8_e4m3fn_x4
+E5M2X4 = mybir.dt.float8_e5m2_x4
+ALU = mybir.AluOpType
+ACT = mybir.ActivationFunctionType
+
+P = 128
+PACK = 4
+K_PASS = P * PACK
+PASSES = DV // K_PASS
+HALF = 512
+UNIT = 256
+QUARTERS = E // UNIT
+D_TILES = D // P
+DIRECT_EDGES = 512
+DIRECT_PIECES = (256, 128, 128)
+
+
+def tile_attend_gmp_ew_kernel(tc, dyT, hE, ew, w_words, w_scales, offs, offs2, out):
+    nc = tc.nc
+    with ExitStack() as ctx:
+        keep = ctx.enter_context(tc.tile_pool(name="keep", bufs=1))
+        psum = ctx.enter_context(tc.psum_pool(name="psum", bufs=1))
+
+        def bank(i, shape):
+            return psum.tile(shape, F32, name="bank%d" % i, tag="bank%d" % i)
+
+        dst = keep.tile([P, E // 16], U16, name="dst")
+        src = keep.tile([P, E // 16], U16, name="src")
+        dy = [[keep.tile([P, V], F32, name="dy%d%d" % (o, t)) for t in range(PACK)] for o in range(PASSES)]
+        h = [[keep.tile([P, PACK, HALF], F32, name="h%d%d" % (o, a)) for a in range(2)] for o in range(PASSES)]
+        ew_rows = keep.tile([P, P], F32, name="ew_rows")
+        ew_cols = keep.tile([P, E // P], F32, name="ew_cols")
+        ew_wide = keep.tile([P, DIRECT_EDGES], F32, name="ew_wide")
+        w_codes = keep.tile([P, PASSES, D], U32, name="w_codes", align_bytes=64)
+        w_plane = keep.tile([P, PASSES * D], U8, name="w_plane", align_bytes=64)
+        ident = keep.tile([P, P], F32, name="ident")
+        codes = [[keep.tile([P, HALF], U32, name="codes%d%d" % (o, a), align_bytes=64) for a in range(2)] for o in range(PASSES)]
+        plane = [[keep.tile([P, HALF], U8, name="plane%d%d" % (o, a), align_bytes=64) for a in range(2)] for o in range(PASSES)]
+        dm = [keep.tile([P, E], F32, name="dm%d" % j) for j in range(D_TILES)]
+
+        def dy_rows(o, t):
+            return dyT[o * K_PASS : (o + 1) * K_PASS, :].rearrange("(p t) v -> p t v", t=PACK)[:, t, :]
+
+        def h_rows(o, a):
+            return hE[o * K_PASS : (o + 1) * K_PASS, a * HALF : (a + 1) * HALF].rearrange("(p t) e -> p t e", t=PACK)
+
+        make_identity(nc, ident[:])
+        nc.vector.memset(w_plane[:].bitcast(I32), 0)
+        for q in range(4):
+            nc.gpsimd.dma_start(
+                out=w_plane[32 * q : 32 * q + 4, :].bitcast(I32).rearrange("f (o d) -> f o d", o=PASSES),
+                in_=w_scales[:, 4 * q : 4 * q + 4, :].bitcast(I32).rearrange("o f d -> f o d"),
+            )
+
+        nc.sync.dma_start(out=h[0][0][:, 0, :], in_=h_rows(0, 0)[:, 0, :])
+        nc.sync.dma_start(dst[:], offs)
+        nc.sync.dma_start(out=dy[0][0][:], in_=dy_rows(0, 0))
+        for t in range(1, PACK):
+            nc.sync.dma_start(out=h[0][0][:, t, :], in_=h_rows(0, 0)[:, t, :])
+            nc.sync.dma_start(out=dy[0][t][:], in_=dy_rows(0, t))
+        nc.sync.dma_start(out=ew_rows[:], in_=ew.rearrange("r (b c) -> (r b) c", c=P)[0:P, :])
+        nc.sync.dma_start(out=h[0][1][:], in_=h_rows(0, 1))
+        nc.sync.dma_start(out=h[1][0][:], in_=h_rows(1, 0))
+        for t in range(PACK):
+            nc.sync.dma_start(out=dy[1][t][:], in_=dy_rows(1, t))
+        nc.sync.dma_start(out=w_codes[:].bitcast(I32), in_=w_words.rearrange("o p d r -> p o (d r)").bitcast(I32))
+        nc.sync.dma_start(out=h[1][1][:], in_=h_rows(1, 1))
+        nc.sync.dma_start(out=ew_wide[:], in_=ew[:, E - DIRECT_EDGES : E])
+        nc.sync.dma_start(src[:], offs2)
+
+        ew_bank = bank(7, [P, P])
+        nc.tensor.transpose(ew_bank[:], ew_rows[:], ident[:])
+        nc.vector.tensor_copy(out=ew_cols[:], in_=ew_bank[:, 0 : E // P])
+
+        def dst_cols(e0, n):
+            return dst[:, e0 // 16 : (e0 + n) // 16]
+
+        def h_piece(o, e0, n):
+            return h[o][e0 // HALF][:, :, e0 % HALF : e0 % HALF + n]
+
+        def quantize(o, e0, n, woven):
+            cols = slice(e0 % HALF, e0 % HALF + n)
+            nc.vector.quantize_mx(
+                out=codes[o][e0 // HALF][:, cols].bitcast(E5M2X4), scales=plane[o][e0 // HALF][:, cols], in_=woven
+            )
+
+        turned = [(o, q * UNIT) for o in range(PASSES) for q in range(QUARTERS)][: (PASSES * E - DIRECT_EDGES) // UNIT]
+        slope = [keep.tile([P, PACK, UNIT], F32, name="slope%d" % i) for i in range(len(turned))]
+        prod = [keep.tile([P, PACK, UNIT], F32, name="prod%d" % i) for i in range(len(turned))]
+        pairs = {}
+        woven = {}
+
+        def relu(i, planes):
+            o, e0 = turned[i]
+            nc.scalar.activation(out=slope[i][:, planes, :], in_=h_piece(o, e0, UNIT)[:, planes, :], func=ACT.Relu, scale=2.0)
+
+        def gather(i, t):
+            o, e0 = turned[i]
+            nc.vector.tensor_tensor(prod[i][:, t, :], dy[o][t][:].indirect(dst_cols(e0, UNIT)), slope[i][:, t, :], ALU.mult)
+
+        def weigh(i):
+            o, e0 = turned[i]
+            for b in range(UNIT // P):
+                by_edge = bank(2 * (i % 2) + b, [P, PACK, P])
+                for t in range(PACK):
+                    nc.tensor.transpose(by_edge[:, t, :], prod[i][:, t, b * P : (b + 1) * P], ident[:])
+                pairs[i, b] = keep.tile([P, 2, P, 2], BF16, name="pairs%d%d" % (i, b))
+                col = e0 // P + b
+                nc.scalar.activation(
+                    out=pairs[i, b][:],
+                    in_=by_edge[:].rearrange("e (u s) p -> e u p s", s=2),
+                    func=ACT.Copy,
+                    scale=ew_cols[:, col : col + 1],
+                )
+
+        def turn_back(i):
+            o, e0 = turned[i]
+            by_row = bank(4 + i % 2, [P, UNIT // P, 2, P])
+            for b in range(UNIT // P):
+                words = pairs[i, b][:].rearrange("e u p s -> e (u p s)").bitcast(F32)
+                for u in range(2):
+                    nc.tensor.transpose(by_row[:, b, u, :], words[:, u * P : (u + 1) * P], ident[:])
+            woven[i] = keep.tile([P, UNIT * PACK], BF16, name="woven%d" % i, align_bytes=64)
+            nc.scalar.copy(
+                out=woven[i][:].bitcast(F32).rearrange("p (b e u) -> p b e u", b=UNIT // P, u=2),
+                in_=by_row[:].rearrange("p b u e -> p b e u"),
+            )
+            quantize(o, e0, UNIT, woven[i][:])
+
+        def direct(e0, n, last):
+            o = PASSES - 1
+            c0 = e0 - (E - DIRECT_EDGES)
+            weighed = keep.tile([P, PACK, n], F32, name="weighed%d" % e0)
+            rounded = keep.tile([P, PACK, n], BF16, name="rounded%d" % e0)
+            woven_direct = keep.tile([P, n, PACK], BF16, name="woven_direct%d" % e0, align_bytes=64)
+            step = 2 if last else PACK
+            for t0 in range(0, PACK, step):
+                for t in range(t0, t0 + step):
+                    nc.vector.tensor_tensor(
+                        weighed[:, t, :], dy[o][t][:].indirect(dst_cols(e0, n)), ew_wide[:, c0 : c0 + n], ALU.mult
+                    )
+            for t0 in range(0, PACK, step):
+                nc.vector.scalar_tensor_tensor(
+                    out=rounded[:, t0 : t0 + step, :],
+                    in0=h_piece(o, e0, n)[:, t0 : t0 + step, :],
+                    scalar=0.0,
+                    in1=weighed[:, t0 : t0 + step, :],
+                    op0=ALU.max,
+                    op1=ALU.mult,
+                )
+            if last:
+                nc.vector.tensor_scalar_mul(woven_direct[:], rounded[:].rearrange("p t e -> p e t"), 2.0)
+            else:
+                nc.scalar.activation(out=woven_direct[:], in_=rounded[:].rearrange("p t e -> p e t"), func=ACT.Copy, scale=2.0)
+            quantize(o, e0, n, woven_direct[:].rearrange("p e t -> p (e t)"))
+
+        def multiply(acc, j, o, a):
+            nc.tensor.matmul_mx(
+                out=acc[:],
+                lhsT=w_codes[:, o, j * P : (j + 1) * P].bitcast(E4M3X4),
+                lhsT_scale=w_plane[:, o * D + j * P : o * D + (j + 1) * P],
+                rhs=codes[o][a][:].bitcast(E5M2X4),
+                rhs_scale=plane[o][a][:],
+                start=(o == 0),
+                stop=(o == PASSES - 1),
+            )
+
+        def first_half():
+            for j in range(D_TILES):
+                acc = bank(6 + j % 2, [P, HALF])
+                for o in range(PASSES):
+                    multiply(acc, j, o, 0)
+                nc.scalar.copy(out=dm[j][:, 0:HALF], in_=acc[:])
+
+        for t in range(PACK):
+            for i in range(2):
+                relu(i, slice(t, t + 1))
+                gather(i, t)
+        n_turned = len(turned)
+        for s in range(2, n_turned + 3):
+            if s < n_turned:
+                relu(s, slice(0, PACK))
+                for t in range(PACK):
+                    gather(s, t)
+            if 0 <= s - 2 < n_turned:
+                weigh(s - 2)
+            if 0 <= s - 3 < n_turned:
+                turn_back(s - 3)
+                if turned[s - 3] == (PASSES - 1, HALF - UNIT):
+                    first_half()
+        e0 = E - DIRECT_EDGES
+        accs = [bank(j, [P, HALF]) for j in range(D_TILES)]
+        for j in range(D_TILES):
+            multiply(accs[j], j, 0, 1)
+        for k, n in enumerate(DIRECT_PIECES):
+            direct(e0, n, k == len(DIRECT_PIECES) - 1)
+            e0 = e0 + n
+        for j in range(D_TILES):
+            multiply(accs[j], j, PASSES - 1, 1)
+            if j == 0:
+                nc.vector.tensor_copy(out=dm[j][:, HALF:E], in_=accs[j][:])
+            else:
+                nc.scalar.copy(out=dm[j][:, HALF:E], in_=accs[j][:])
+
+        for j in range(D_TILES):
+            looked = keep.tile([P, E], F32, name="looked%d" % j)
+            summed = keep.tile([P, V], F32, name="summed%d" % j)
+            for a in range(2):
+                nc.vector.tensor_copy(
+                    looked[:, a * HALF : (a + 1) * HALF], dm[j][:].indirect(src[:, a * HALF // 16 : (a + 1) * HALF // 16])
+                )
+            for a in range(2):
+                both = looked[:, a * HALF : (a + 1) * HALF].rearrange("p (x k) -> p x k", k=K)
+                nodes = slice(a * V // 2, (a + 1) * V // 2)
+                nc.vector.tensor_tensor(summed[:, nodes], both[:, :, 0], both[:, :, 1], ALU.add)
+                if j == D_TILES - 1:
+                    nc.sync.dma_start(out=out[j * P : (j + 1) * P, nodes], in_=summed[:, nodes])
+            if j < D_TILES - 1:
+                nc.sync.dma_start(out=out[j * P : (j + 1) * P, :], in_=summed[:])

@@ -25,8 +25,10 @@ HALF = 512
 UNIT = 256
 QUARTERS = E // UNIT
 D_TILES = D // P
+SPARE = 16
+DM_SPARE = 352
 DIRECT_EDGES = 512
-DIRECT_PIECES = (256, 128, 128)
+DIRECT_PIECES = (384, 128)
 
 
 def tile_attend_gmp_ew_kernel(tc, dyT, hE, ew, w_words, w_scales, offs, offs2, out):
@@ -40,7 +42,7 @@ def tile_attend_gmp_ew_kernel(tc, dyT, hE, ew, w_words, w_scales, offs, offs2, o
 
         dst = keep.tile([P, E // 16], U16, name="dst")
         src = keep.tile([P, E // 16], U16, name="src")
-        dy = [[keep.tile([P, V], F32, name="dy%d%d" % (o, t)) for t in range(PACK)] for o in range(PASSES)]
+        dy = [[keep.tile([P, V + SPARE], F32, name="dy%d%d" % (o, t)) for t in range(PACK)] for o in range(PASSES)]
         h = [[keep.tile([P, PACK, HALF], F32, name="h%d%d" % (o, a)) for a in range(2)] for o in range(PASSES)]
         ew_rows = keep.tile([P, P], F32, name="ew_rows")
         ew_cols = keep.tile([P, E // P], F32, name="ew_cols")
@@ -50,7 +52,7 @@ def tile_attend_gmp_ew_kernel(tc, dyT, hE, ew, w_words, w_scales, offs, offs2, o
         ident = keep.tile([P, P], F32, name="ident")
         codes = [[keep.tile([P, HALF], U32, name="codes%d%d" % (o, a), align_bytes=64) for a in range(2)] for o in range(PASSES)]
         plane = [[keep.tile([P, HALF], U8, name="plane%d%d" % (o, a), align_bytes=64) for a in range(2)] for o in range(PASSES)]
-        dm = [keep.tile([P, E], F32, name="dm%d" % j) for j in range(D_TILES)]
+        dm = [keep.tile([P, E + (DM_SPARE if j < D_TILES - 1 else 0)], F32, name="dm%d" % j) for j in range(D_TILES)]
 
         def dy_rows(o, t):
             return dyT[o * K_PASS : (o + 1) * K_PASS, :].rearrange("(p t) v -> p t v", t=PACK)[:, t, :]
@@ -66,20 +68,27 @@ def tile_attend_gmp_ew_kernel(tc, dyT, hE, ew, w_words, w_scales, offs, offs2, o
                 in_=w_scales[:, 4 * q : 4 * q + 4, :].bitcast(I32).rearrange("o f d -> f o d"),
             )
 
+        for o in range(PASSES):
+            for t in range(PACK):
+                nc.vector.memset(dy[o][t][:, V:], 0.0)
+        for j in range(D_TILES - 1):
+            nc.vector.memset(dm[j][:, E:], 0.0)
+
         nc.sync.dma_start(out=h[0][0][:, 0, :], in_=h_rows(0, 0)[:, 0, :])
         nc.sync.dma_start(dst[:], offs)
-        nc.sync.dma_start(out=dy[0][0][:], in_=dy_rows(0, 0))
+        nc.sync.dma_start(out=dy[0][0][:, 0:V], in_=dy_rows(0, 0))
         for t in range(1, PACK):
             nc.sync.dma_start(out=h[0][0][:, t, :], in_=h_rows(0, 0)[:, t, :])
-            nc.sync.dma_start(out=dy[0][t][:], in_=dy_rows(0, t))
+            nc.sync.dma_start(out=dy[0][t][:, 0:V], in_=dy_rows(0, t))
         nc.sync.dma_start(out=ew_rows[:], in_=ew.rearrange("r (b c) -> (r b) c", c=P)[0:P, :])
-        nc.sync.dma_start(out=h[0][1][:], in_=h_rows(0, 1))
+        for t in range(0, PACK, 2):
+            nc.sync.dma_start(out=h[0][1][:, t : t + 2, :], in_=h_rows(0, 1)[:, t : t + 2, :])
         nc.sync.dma_start(out=h[1][0][:], in_=h_rows(1, 0))
         for t in range(PACK):
-            nc.sync.dma_start(out=dy[1][t][:], in_=dy_rows(1, t))
-        nc.sync.dma_start(out=w_codes[:].bitcast(I32), in_=w_words.rearrange("o p d r -> p o (d r)").bitcast(I32))
-        nc.sync.dma_start(out=h[1][1][:], in_=h_rows(1, 1))
+            nc.sync.dma_start(out=dy[1][t][:, 0:V], in_=dy_rows(1, t))
         nc.sync.dma_start(out=ew_wide[:], in_=ew[:, E - DIRECT_EDGES : E])
+        nc.sync.dma_start(out=h[1][1][:], in_=h_rows(1, 1))
+        nc.sync.dma_start(out=w_codes[:].bitcast(I32), in_=w_words.rearrange("o p d r -> p o (d r)").bitcast(I32))
         nc.sync.dma_start(src[:], offs2)
 
         ew_bank = bank(7, [P, P])
@@ -98,61 +107,66 @@ def tile_attend_gmp_ew_kernel(tc, dyT, hE, ew, w_words, w_scales, offs, offs2, o
                 out=codes[o][e0 // HALF][:, cols].bitcast(E5M2X4), scales=plane[o][e0 // HALF][:, cols], in_=woven
             )
 
-        turned = [(o, q * UNIT) for o in range(PASSES) for q in range(QUARTERS)][: (PASSES * E - DIRECT_EDGES) // UNIT]
-        slope = [keep.tile([P, PACK, UNIT], F32, name="slope%d" % i) for i in range(len(turned))]
-        prod = [keep.tile([P, PACK, UNIT], F32, name="prod%d" % i) for i in range(len(turned))]
-        pairs = {}
-        woven = {}
+        turned = [(0, 0), (0, 1), (1, 0)]
+        slope = [keep.tile([P, PACK, HALF], F32, name="slope%d" % i) for i in range(len(turned))]
+        prod = [keep.tile([P, PACK, HALF], F32, name="prod%d" % i) for i in range(len(turned))]
+        BLOCKS = HALF // P
 
-        def relu(i, planes):
-            o, e0 = turned[i]
-            nc.scalar.activation(out=slope[i][:, planes, :], in_=h_piece(o, e0, UNIT)[:, planes, :], func=ACT.Relu, scale=2.0)
+        def relu(i):
+            o, a = turned[i]
+            for t in range(PACK):
+                nc.scalar.activation(out=slope[i][:, t, :], in_=h[o][a][:, t, :], func=ACT.Relu, scale=2.0)
 
-        def gather(i, t):
-            o, e0 = turned[i]
-            nc.vector.tensor_tensor(prod[i][:, t, :], dy[o][t][:].indirect(dst_cols(e0, UNIT)), slope[i][:, t, :], ALU.mult)
+        def gather_and_turn(i):
+            o, a = turned[i]
+            by_edge = psum.tile([P, BLOCKS, PACK, P], F32, name="wide", tag="wide")
+            for t in range(PACK):
+                nc.vector.tensor_tensor(prod[i][:, t, :], dy[o][t][:].indirect(dst_cols(a * HALF, HALF)), slope[i][:, t, :], ALU.mult)
+                for b in range(BLOCKS):
+                    nc.tensor.transpose(by_edge[:, b, t, :], prod[i][:, t, b * P : (b + 1) * P], ident[:])
+            return by_edge
 
-        def weigh(i):
-            o, e0 = turned[i]
-            for b in range(UNIT // P):
-                by_edge = bank(2 * (i % 2) + b, [P, PACK, P])
-                for t in range(PACK):
-                    nc.tensor.transpose(by_edge[:, t, :], prod[i][:, t, b * P : (b + 1) * P], ident[:])
-                pairs[i, b] = keep.tile([P, 2, P, 2], BF16, name="pairs%d%d" % (i, b))
-                col = e0 // P + b
-                nc.scalar.activation(
-                    out=pairs[i, b][:],
-                    in_=by_edge[:].rearrange("e (u s) p -> e u p s", s=2),
-                    func=ACT.Copy,
-                    scale=ew_cols[:, col : col + 1],
+        def weigh_and_turn_back(i, by_edge):
+            o, a = turned[i]
+            for g in range(2):
+                by_row = bank(4 + g, [P, 2, 2, P])
+                for b in range(2):
+                    pairs = keep.tile([P, 2, P, 2], BF16, name="pairs%d%d%d" % (i, g, b))
+                    col = a * BLOCKS + 2 * g + b
+                    nc.scalar.activation(
+                        out=pairs[:],
+                        in_=by_edge[:, 2 * g + b].rearrange("e (u s) p -> e u p s", s=2),
+                        func=ACT.Copy,
+                        scale=ew_cols[:, col : col + 1],
+                    )
+                    words = pairs[:].rearrange("e u p s -> e (u p s)").bitcast(F32)
+                    for u in range(2):
+                        nc.tensor.transpose(by_row[:, b, u, :], words[:, u * P : (u + 1) * P], ident[:])
+                rows.append(by_row)
+
+        def weave(i):
+            o, a = turned[i]
+            for g in range(2):
+                woven = keep.tile([P, UNIT * PACK], BF16, name="woven%d%d" % (i, g), tag="woven%d%d" % (i, g), align_bytes=64)
+                nc.scalar.copy(
+                    out=woven[:].bitcast(F32).rearrange("p (b e u) -> p b e u", b=2, u=2),
+                    in_=rows[2 * i + g][:].rearrange("p b u e -> p b e u"),
                 )
-
-        def turn_back(i):
-            o, e0 = turned[i]
-            by_row = bank(4 + i % 2, [P, UNIT // P, 2, P])
-            for b in range(UNIT // P):
-                words = pairs[i, b][:].rearrange("e u p s -> e (u p s)").bitcast(F32)
-                for u in range(2):
-                    nc.tensor.transpose(by_row[:, b, u, :], words[:, u * P : (u + 1) * P], ident[:])
-            woven[i] = keep.tile([P, UNIT * PACK], BF16, name="woven%d" % i, align_bytes=64)
-            nc.scalar.copy(
-                out=woven[i][:].bitcast(F32).rearrange("p (b e u) -> p b e u", b=UNIT // P, u=2),
-                in_=by_row[:].rearrange("p b u e -> p b e u"),
-            )
-            quantize(o, e0, UNIT, woven[i][:])
+                quantize(o, a * HALF + g * UNIT, UNIT, woven[:])
 
         def direct(e0, n, last):
             o = PASSES - 1
             c0 = e0 - (E - DIRECT_EDGES)
-            weighed = keep.tile([P, PACK, n], F32, name="weighed%d" % e0)
+            weighed = keep.tile([P, PACK, n], F32, name="weighed%d" % e0, tag="woven20" if last else "woven11", align_bytes=64)
             rounded = keep.tile([P, PACK, n], BF16, name="rounded%d" % e0)
-            woven_direct = keep.tile([P, n, PACK], BF16, name="woven_direct%d" % e0, align_bytes=64)
+            woven_direct = keep.tile(
+                [P, n, PACK], BF16, name="woven_direct%d" % e0, tag="woven_last" if last else "woven21", align_bytes=64
+            )
             step = 2 if last else PACK
-            for t0 in range(0, PACK, step):
-                for t in range(t0, t0 + step):
-                    nc.vector.tensor_tensor(
-                        weighed[:, t, :], dy[o][t][:].indirect(dst_cols(e0, n)), ew_wide[:, c0 : c0 + n], ALU.mult
-                    )
+            for t in range(PACK):
+                nc.vector.tensor_tensor(
+                    weighed[:, t, :], dy[o][t][:].indirect(dst_cols(e0, n)), ew_wide[:, c0 : c0 + n], ALU.mult
+                )
             for t0 in range(0, PACK, step):
                 nc.vector.scalar_tensor_tensor(
                     out=rounded[:, t0 : t0 + step, :],
@@ -164,13 +178,20 @@ def tile_attend_gmp_ew_kernel(tc, dyT, hE, ew, w_words, w_scales, offs, offs2, o
                 )
             if last:
                 nc.vector.tensor_scalar_mul(woven_direct[:], rounded[:].rearrange("p t e -> p e t"), 2.0)
+                quantize(o, e0, n, woven_direct[:].rearrange("p e t -> p (e t)"))
             else:
-                nc.scalar.activation(out=woven_direct[:], in_=rounded[:].rearrange("p t e -> p e t"), func=ACT.Copy, scale=2.0)
-            quantize(o, e0, n, woven_direct[:].rearrange("p e t -> p (e t)"))
+                for x0, m in ((0, UNIT), (UNIT, n - UNIT)):
+                    nc.scalar.activation(
+                        out=woven_direct[:, x0 : x0 + m, :],
+                        in_=rounded[:, :, x0 : x0 + m].rearrange("p t e -> p e t"),
+                        func=ACT.Copy,
+                        scale=2.0,
+                    )
+                    quantize(o, e0 + x0, m, woven_direct[:, x0 : x0 + m, :].rearrange("p e t -> p (e t)"))
 
         def multiply(acc, j, o, a):
             nc.tensor.matmul_mx(
-                out=acc[:],
+                out=acc,
                 lhsT=w_codes[:, o, j * P : (j + 1) * P].bitcast(E4M3X4),
                 lhsT_scale=w_plane[:, o * D + j * P : o * D + (j + 1) * P],
                 rhs=codes[o][a][:].bitcast(E5M2X4),
@@ -179,55 +200,56 @@ def tile_attend_gmp_ew_kernel(tc, dyT, hE, ew, w_words, w_scales, offs, offs2, o
                 stop=(o == PASSES - 1),
             )
 
-        def first_half():
-            for j in range(D_TILES):
-                acc = bank(6 + j % 2, [P, HALF])
-                for o in range(PASSES):
-                    multiply(acc, j, o, 0)
-                nc.scalar.copy(out=dm[j][:, 0:HALF], in_=acc[:])
-
-        for t in range(PACK):
-            for i in range(2):
-                relu(i, slice(t, t + 1))
-                gather(i, t)
-        n_turned = len(turned)
-        for s in range(2, n_turned + 3):
-            if s < n_turned:
-                relu(s, slice(0, PACK))
-                for t in range(PACK):
-                    gather(s, t)
-            if 0 <= s - 2 < n_turned:
-                weigh(s - 2)
-            if 0 <= s - 3 < n_turned:
-                turn_back(s - 3)
-                if turned[s - 3] == (PASSES - 1, HALF - UNIT):
-                    first_half()
-        e0 = E - DIRECT_EDGES
-        accs = [bank(j, [P, HALF]) for j in range(D_TILES)]
+        rows = []
+        relu(0)
+        by_edge = gather_and_turn(0)
+        for i in range(len(turned)):
+            if i + 1 < len(turned):
+                relu(i + 1)
+            weigh_and_turn_back(i, by_edge)
+            weave(i)
+            if i + 1 < len(turned):
+                by_edge = gather_and_turn(i + 1)
+        late = psum.tile([P, D_TILES, HALF], F32, name="wide", tag="wide")
         for j in range(D_TILES):
-            multiply(accs[j], j, 0, 1)
+            multiply(late[:, j, :], j, 0, 1)
+        early = [bank(b, [P, HALF]) for b in (6, 7, 4, 5)]
+        for j in range(D_TILES):
+            for o in range(PASSES):
+                multiply(early[j][:], j, o, 0)
+        e0 = E - DIRECT_EDGES
         for k, n in enumerate(DIRECT_PIECES):
             direct(e0, n, k == len(DIRECT_PIECES) - 1)
             e0 = e0 + n
         for j in range(D_TILES):
-            multiply(accs[j], j, PASSES - 1, 1)
+            multiply(late[:, j, :], j, PASSES - 1, 1)
+            nc.scalar.copy(out=dm[j][:, 0:HALF], in_=early[j][:])
             if j == 0:
-                nc.vector.tensor_copy(out=dm[j][:, HALF:E], in_=accs[j][:])
+                nc.vector.tensor_copy(out=dm[j][:, HALF:E], in_=late[:, j, :])
             else:
-                nc.scalar.copy(out=dm[j][:, HALF:E], in_=accs[j][:])
+                nc.scalar.copy(out=dm[j][:, HALF:E], in_=late[:, j, :])
 
         for j in range(D_TILES):
             looked = keep.tile([P, E], F32, name="looked%d" % j)
             summed = keep.tile([P, V], F32, name="summed%d" % j)
-            for a in range(2):
-                nc.vector.tensor_copy(
-                    looked[:, a * HALF : (a + 1) * HALF], dm[j][:].indirect(src[:, a * HALF // 16 : (a + 1) * HALF // 16])
-                )
-            for a in range(2):
-                both = looked[:, a * HALF : (a + 1) * HALF].rearrange("p (x k) -> p x k", k=K)
-                nodes = slice(a * V // 2, (a + 1) * V // 2)
-                nc.vector.tensor_tensor(summed[:, nodes], both[:, :, 0], both[:, :, 1], ALU.add)
-                if j == D_TILES - 1:
-                    nc.sync.dma_start(out=out[j * P : (j + 1) * P, nodes], in_=summed[:, nodes])
-            if j < D_TILES - 1:
-                nc.sync.dma_start(out=out[j * P : (j + 1) * P, :], in_=summed[:])
+            cuts = (0, E) if j < D_TILES - 1 else (0, 512, 768, E)
+            for c0, c1 in zip(cuts[:-1], cuts[1:]):
+                nc.vector.tensor_copy(looked[:, c0:c1], dm[j][:].indirect(src[:, c0 // 16 : c1 // 16]))
+                both = looked[:, c0:c1].rearrange("p (x k) -> p x k", k=K)
+                nodes = slice(c0 // K, c1 // K)
+                if j < 2:
+                    by_node = bank((6, 4)[j], [P, V // P, P])
+                    for b in range(V // P):
+                        for k in range(K):
+                            nc.tensor.matmul(
+                                by_node[:, b, :], both[:, b * P : (b + 1) * P, k], ident[:], start=(k == 0), stop=(k == K - 1), is_transpose=True
+                            )
+                    sums = keep.tile([P, V // P, P], F32, name="sums%d" % j)
+                    nc.scalar.copy(out=sums[:], in_=by_node[:])
+                    by_feature = bank((7, 5)[j], [P, V // P, P])
+                    for b in range(V // P):
+                        nc.tensor.transpose(by_feature[:, b, :], sums[:, b, :], ident[:])
+                    nc.scalar.copy(out=summed[:], in_=by_feature[:].rearrange("p b x -> p (b x)"))
+                else:
+                    nc.vector.tensor_tensor(summed[:, nodes], both[:, :, 0], both[:, :, 1], ALU.add)
+                nc.sync.dma_start(out=out[j * P : (j + 1) * P, nodes], in_=summed[:, nodes])

@@ -27,8 +27,7 @@ QUARTERS = E // UNIT
 D_TILES = D // P
 SPARE = 16
 DM_SPARE = 352
-DIRECT_EDGES = 512
-DIRECT_PIECES = (384, 128)
+DIRECT_EDGES = 128
 
 
 def tile_attend_gmp_ew_kernel(tc, dyT, hE, ew, w_words, w_scales, offs, offs2, out):
@@ -62,12 +61,6 @@ def tile_attend_gmp_ew_kernel(tc, dyT, hE, ew, w_words, w_scales, offs, offs2, o
 
         make_identity(nc, ident[:])
         nc.vector.memset(w_plane[:].bitcast(I32), 0)
-        for q in range(4):
-            nc.gpsimd.dma_start(
-                out=w_plane[32 * q : 32 * q + 4, :].bitcast(I32).rearrange("f (o d) -> f o d", o=PASSES),
-                in_=w_scales[:, 4 * q : 4 * q + 4, :].bitcast(I32).rearrange("o f d -> f o d"),
-            )
-
         for o in range(PASSES):
             for t in range(PACK):
                 nc.vector.memset(dy[o][t][:, V:], 0.0)
@@ -86,9 +79,14 @@ def tile_attend_gmp_ew_kernel(tc, dyT, hE, ew, w_words, w_scales, offs, offs2, o
         nc.sync.dma_start(out=h[1][0][:], in_=h_rows(1, 0))
         for t in range(PACK):
             nc.sync.dma_start(out=dy[1][t][:, 0:V], in_=dy_rows(1, t))
-        nc.sync.dma_start(out=ew_wide[:], in_=ew[:, E - DIRECT_EDGES : E])
         nc.sync.dma_start(out=h[1][1][:], in_=h_rows(1, 1))
+        nc.sync.dma_start(out=ew_wide[:], in_=ew[:, E - DIRECT_EDGES : E])
         nc.sync.dma_start(out=w_codes[:].bitcast(I32), in_=w_words.rearrange("o p d r -> p o (d r)").bitcast(I32))
+        for q in range(4):
+            nc.sync.dma_start(
+                out=w_plane[32 * q : 32 * q + 4, :].bitcast(I32).rearrange("f (o d) -> f o d", o=PASSES),
+                in_=w_scales[:, 4 * q : 4 * q + 4, :].bitcast(I32).rearrange("o f d -> f o d"),
+            )
         nc.sync.dma_start(src[:], offs2)
 
         ew_bank = bank(7, [P, P])
@@ -107,87 +105,71 @@ def tile_attend_gmp_ew_kernel(tc, dyT, hE, ew, w_words, w_scales, offs, offs2, o
                 out=codes[o][e0 // HALF][:, cols].bitcast(E5M2X4), scales=plane[o][e0 // HALF][:, cols], in_=woven
             )
 
-        turned = [(0, 0), (0, 1), (1, 0)]
-        slope = [keep.tile([P, PACK, HALF], F32, name="slope%d" % i) for i in range(len(turned))]
-        prod = [keep.tile([P, PACK, HALF], F32, name="prod%d" % i) for i in range(len(turned))]
-        BLOCKS = HALF // P
+        turned = [(0, 0, HALF), (0, 1, HALF), (1, 0, HALF), (1, 1, HALF - DIRECT_EDGES)]
+        slope = [keep.tile([P, PACK, n], F32, name="slope%d" % i) for i, (o, a, n) in enumerate(turned)]
+        prod = [keep.tile([P, PACK, n], F32, name="prod%d" % i) for i, (o, a, n) in enumerate(turned)]
 
         def relu(i):
-            o, a = turned[i]
+            o, a, n = turned[i]
             for t in range(PACK):
-                nc.scalar.activation(out=slope[i][:, t, :], in_=h[o][a][:, t, :], func=ACT.Relu, scale=2.0)
+                nc.scalar.activation(out=slope[i][:, t, :], in_=h[o][a][:, t, 0:n], func=ACT.Relu, scale=2.0)
 
         def gather_and_turn(i):
-            o, a = turned[i]
-            by_edge = psum.tile([P, BLOCKS, PACK, P], F32, name="wide", tag="wide")
+            o, a, n = turned[i]
+            by_edge = psum.tile([P, n // P, PACK, P], F32, name="wide", tag="wide")
             for t in range(PACK):
-                nc.vector.tensor_tensor(prod[i][:, t, :], dy[o][t][:].indirect(dst_cols(a * HALF, HALF)), slope[i][:, t, :], ALU.mult)
-                for b in range(BLOCKS):
+                nc.vector.tensor_tensor(prod[i][:, t, :], dy[o][t][:].indirect(dst_cols(a * HALF, n)), slope[i][:, t, :], ALU.mult)
+                for b in range(n // P):
                     nc.tensor.transpose(by_edge[:, b, t, :], prod[i][:, t, b * P : (b + 1) * P], ident[:])
             return by_edge
 
-        def weigh_and_turn_back(i, by_edge):
-            o, a = turned[i]
-            for g in range(2):
-                by_row = bank(4 + g, [P, 2, 2, P])
-                for b in range(2):
-                    pairs = keep.tile([P, 2, P, 2], BF16, name="pairs%d%d%d" % (i, g, b))
-                    col = a * BLOCKS + 2 * g + b
+        def weigh_and_weave(i, by_edge):
+            o, a, n = turned[i]
+            groups = [range(b0, min(b0 + 2, n // P)) for b0 in range(0, n // P, 2)]
+            rows = []
+            for g, blocks in enumerate(groups):
+                by_row = bank(4 + g, [P, len(blocks), 2, P])
+                for b in blocks:
+                    pairs = keep.tile([P, 2, P, 2], BF16, name="pairs%d%d" % (i, b))
+                    col = a * (HALF // P) + b
                     nc.scalar.activation(
                         out=pairs[:],
-                        in_=by_edge[:, 2 * g + b].rearrange("e (u s) p -> e u p s", s=2),
+                        in_=by_edge[:, b].rearrange("e (u s) p -> e u p s", s=2),
                         func=ACT.Copy,
                         scale=ew_cols[:, col : col + 1],
                     )
                     words = pairs[:].rearrange("e u p s -> e (u p s)").bitcast(F32)
                     for u in range(2):
-                        nc.tensor.transpose(by_row[:, b, u, :], words[:, u * P : (u + 1) * P], ident[:])
+                        nc.tensor.transpose(by_row[:, b % 2, u, :], words[:, u * P : (u + 1) * P], ident[:])
                 rows.append(by_row)
-
-        def weave(i):
-            o, a = turned[i]
-            for g in range(2):
-                woven = keep.tile([P, UNIT * PACK], BF16, name="woven%d%d" % (i, g), tag="woven%d%d" % (i, g), align_bytes=64)
+            for g, blocks in enumerate(groups):
+                width = len(blocks) * P
+                woven = keep.tile([P, width * PACK], BF16, name="woven%d%d" % (i, g), tag="woven%d%d" % (i, g), align_bytes=64)
                 nc.scalar.copy(
-                    out=woven[:].bitcast(F32).rearrange("p (b e u) -> p b e u", b=2, u=2),
-                    in_=rows[2 * i + g][:].rearrange("p b u e -> p b e u"),
+                    out=woven[:].bitcast(F32).rearrange("p (b e u) -> p b e u", b=len(blocks), u=2),
+                    in_=rows[g][:].rearrange("p b u e -> p b e u"),
                 )
-                quantize(o, a * HALF + g * UNIT, UNIT, woven[:])
+                quantize(o, a * HALF + g * UNIT, width, woven[:])
 
-        def direct(e0, n, last):
-            o = PASSES - 1
-            c0 = e0 - (E - DIRECT_EDGES)
-            weighed = keep.tile([P, PACK, n], F32, name="weighed%d" % e0, tag="woven20" if last else "woven11", align_bytes=64)
-            rounded = keep.tile([P, PACK, n], BF16, name="rounded%d" % e0)
-            woven_direct = keep.tile(
-                [P, n, PACK], BF16, name="woven_direct%d" % e0, tag="woven_last" if last else "woven21", align_bytes=64
-            )
-            step = 2 if last else PACK
+        def direct():
+            o, n = PASSES - 1, DIRECT_EDGES
+            e0 = E - n
+            weighed = keep.tile([P, PACK, n], F32, name="weighed", tag="woven20", align_bytes=64)
+            rounded = keep.tile([P, PACK, n], BF16, name="rounded")
+            woven_direct = keep.tile([P, n, PACK], BF16, name="woven_direct", align_bytes=64)
             for t in range(PACK):
-                nc.vector.tensor_tensor(
-                    weighed[:, t, :], dy[o][t][:].indirect(dst_cols(e0, n)), ew_wide[:, c0 : c0 + n], ALU.mult
-                )
-            for t0 in range(0, PACK, step):
+                nc.vector.tensor_tensor(weighed[:, t, :], dy[o][t][:].indirect(dst_cols(e0, n)), ew_wide[:], ALU.mult)
+            for t0 in range(0, PACK, 2):
                 nc.vector.scalar_tensor_tensor(
-                    out=rounded[:, t0 : t0 + step, :],
-                    in0=h_piece(o, e0, n)[:, t0 : t0 + step, :],
+                    out=rounded[:, t0 : t0 + 2, :],
+                    in0=h_piece(o, e0, n)[:, t0 : t0 + 2, :],
                     scalar=0.0,
-                    in1=weighed[:, t0 : t0 + step, :],
+                    in1=weighed[:, t0 : t0 + 2, :],
                     op0=ALU.max,
                     op1=ALU.mult,
                 )
-            if last:
-                nc.vector.tensor_scalar_mul(woven_direct[:], rounded[:].rearrange("p t e -> p e t"), 2.0)
-                quantize(o, e0, n, woven_direct[:].rearrange("p e t -> p (e t)"))
-            else:
-                for x0, m in ((0, UNIT), (UNIT, n - UNIT)):
-                    nc.scalar.activation(
-                        out=woven_direct[:, x0 : x0 + m, :],
-                        in_=rounded[:, :, x0 : x0 + m].rearrange("p t e -> p e t"),
-                        func=ACT.Copy,
-                        scale=2.0,
-                    )
-                    quantize(o, e0 + x0, m, woven_direct[:, x0 : x0 + m, :].rearrange("p e t -> p (e t)"))
+            nc.vector.tensor_scalar_mul(woven_direct[:], rounded[:].rearrange("p t e -> p e t"), 2.0)
+            quantize(o, e0, n, woven_direct[:].rearrange("p e t -> p (e t)"))
 
         def multiply(acc, j, o, a):
             nc.tensor.matmul_mx(
@@ -200,34 +182,31 @@ def tile_attend_gmp_ew_kernel(tc, dyT, hE, ew, w_words, w_scales, offs, offs2, o
                 stop=(o == PASSES - 1),
             )
 
-        rows = []
         relu(0)
         by_edge = gather_and_turn(0)
         for i in range(len(turned)):
-            if i + 1 < len(turned):
-                relu(i + 1)
-            weigh_and_turn_back(i, by_edge)
-            weave(i)
+            if i == 0:
+                relu(1)
+            weigh_and_weave(i, by_edge)
+            if i + 2 < len(turned):
+                relu(i + 2)
             if i + 1 < len(turned):
                 by_edge = gather_and_turn(i + 1)
-        late = psum.tile([P, D_TILES, HALF], F32, name="wide", tag="wide")
+        direct()
         for j in range(D_TILES):
-            multiply(late[:, j, :], j, 0, 1)
-        early = [bank(b, [P, HALF]) for b in (6, 7, 4, 5)]
-        for j in range(D_TILES):
-            for o in range(PASSES):
-                multiply(early[j][:], j, o, 0)
-        e0 = E - DIRECT_EDGES
-        for k, n in enumerate(DIRECT_PIECES):
-            direct(e0, n, k == len(DIRECT_PIECES) - 1)
-            e0 = e0 + n
-        for j in range(D_TILES):
-            multiply(late[:, j, :], j, PASSES - 1, 1)
-            nc.scalar.copy(out=dm[j][:, 0:HALF], in_=early[j][:])
-            if j == 0:
-                nc.vector.tensor_copy(out=dm[j][:, HALF:E], in_=late[:, j, :])
+            if j % 2 == 0:
+                accs = [bank(b, [P, HALF])[:] for b in ((6, 7), (7, 6))[j // 2]]
             else:
-                nc.scalar.copy(out=dm[j][:, HALF:E], in_=late[:, j, :])
+                two = psum.tile([P, 2, HALF], F32, name="wide", tag="wide")
+                accs = [two[:, a, :] for a in range(2)]
+            for a in range(2):
+                for o in range(PASSES):
+                    multiply(accs[a], j, o, a)
+            nc.scalar.copy(out=dm[j][:, 0:HALF], in_=accs[0])
+            if j == 0:
+                nc.vector.tensor_copy(out=dm[j][:, HALF:E], in_=accs[1])
+            else:
+                nc.scalar.copy(out=dm[j][:, HALF:E], in_=accs[1])
 
         for j in range(D_TILES):
             looked = keep.tile([P, E], F32, name="looked%d" % j)
@@ -237,8 +216,8 @@ def tile_attend_gmp_ew_kernel(tc, dyT, hE, ew, w_words, w_scales, offs, offs2, o
                 nc.vector.tensor_copy(looked[:, c0:c1], dm[j][:].indirect(src[:, c0 // 16 : c1 // 16]))
                 both = looked[:, c0:c1].rearrange("p (x k) -> p x k", k=K)
                 nodes = slice(c0 // K, c1 // K)
-                if j < 2:
-                    by_node = bank((6, 4)[j], [P, V // P, P])
+                if j == 0:
+                    by_node = bank(4, [P, V // P, P])
                     for b in range(V // P):
                         for k in range(K):
                             nc.tensor.matmul(
@@ -246,7 +225,7 @@ def tile_attend_gmp_ew_kernel(tc, dyT, hE, ew, w_words, w_scales, offs, offs2, o
                             )
                     sums = keep.tile([P, V // P, P], F32, name="sums%d" % j)
                     nc.scalar.copy(out=sums[:], in_=by_node[:])
-                    by_feature = bank((7, 5)[j], [P, V // P, P])
+                    by_feature = bank(5, [P, V // P, P])
                     for b in range(V // P):
                         nc.tensor.transpose(by_feature[:, b, :], sums[:, b, :], ident[:])
                     nc.scalar.copy(out=summed[:], in_=by_feature[:].rearrange("p b x -> p (b x)"))

@@ -119,7 +119,9 @@ def tile_attend_gmp_ew_kernel(tc, dyT, hE, ew, w_words, w_scales, offs, offs2, o
             by_edge = psum.tile([P, n // P, PACK, P], F32, name="wide", tag="wide")
             for t in range(PACK):
                 nc.vector.tensor_tensor(prod[i][:, t, :], dy[o][t][:].indirect(dst_cols(a * HALF, n)), slope[i][:, t, :], ALU.mult)
-                for b in range(n // P):
+            order = [(b, t) for t in range(PACK) for b in range(n // P)]
+            for b, t in (sorted(order) if i >= 3 else order):
+                if True:
                     nc.tensor.transpose(by_edge[:, b, t, :], prod[i][:, t, b * P : (b + 1) * P], ident[:])
             return by_edge
 
@@ -194,11 +196,7 @@ def tile_attend_gmp_ew_kernel(tc, dyT, hE, ew, w_words, w_scales, offs, offs2, o
                 by_edge = gather_and_turn(i + 1)
         direct()
         for j in range(D_TILES):
-            if j % 2 == 0:
-                accs = [bank(b, [P, HALF])[:] for b in ((6, 7), (7, 6))[j // 2]]
-            else:
-                two = psum.tile([P, 2, HALF], F32, name="wide", tag="wide")
-                accs = [two[:, a, :] for a in range(2)]
+            accs = [bank(6 + a, [P, HALF])[:] for a in range(2)]
             for a in range(2):
                 for o in range(PASSES):
                     multiply(accs[a], j, o, a)
@@ -216,19 +214,8 @@ def tile_attend_gmp_ew_kernel(tc, dyT, hE, ew, w_words, w_scales, offs, offs2, o
                 nc.vector.tensor_copy(looked[:, c0:c1], dm[j][:].indirect(src[:, c0 // 16 : c1 // 16]))
                 both = looked[:, c0:c1].rearrange("p (x k) -> p x k", k=K)
                 nodes = slice(c0 // K, c1 // K)
-                if j == 0:
-                    by_node = bank(4, [P, V // P, P])
-                    for b in range(V // P):
-                        for k in range(K):
-                            nc.tensor.matmul(
-                                by_node[:, b, :], both[:, b * P : (b + 1) * P, k], ident[:], start=(k == 0), stop=(k == K - 1), is_transpose=True
-                            )
-                    sums = keep.tile([P, V // P, P], F32, name="sums%d" % j)
-                    nc.scalar.copy(out=sums[:], in_=by_node[:])
-                    by_feature = bank(5, [P, V // P, P])
-                    for b in range(V // P):
-                        nc.tensor.transpose(by_feature[:, b, :], sums[:, b, :], ident[:])
-                    nc.scalar.copy(out=summed[:], in_=by_feature[:].rearrange("p b x -> p (b x)"))
+                if j < D_TILES - 1:
+                    nc.gpsimd.tensor_tensor(summed[:, nodes], both[:, :, 0], both[:, :, 1], ALU.add)
                 else:
                     nc.vector.tensor_tensor(summed[:, nodes], both[:, :, 0], both[:, :, 1], ALU.add)
                 nc.sync.dma_start(out=out[j * P : (j + 1) * P, nodes], in_=summed[:, nodes])

@@ -22,12 +22,15 @@ PACK = 4
 K_PASS = P * PACK
 PASSES = DV // K_PASS
 HALF = 512
-UNIT = 256
-QUARTERS = E // UNIT
+HALVES = E // HALF
 D_TILES = D // P
-SPARE = 16
+PER_COLUMN = 16
+GROUP = 2
+
+DY_SPARE = 16
 DM_SPARE = 352
-DIRECT_EDGES = 128
+DIRECT_EDGES = P
+LAST_CUTS = (0, E // 2, 3 * E // 4, E)
 
 
 def tile_attend_gmp_ew_kernel(tc, dyT, hE, ew, w_words, w_scales, offs, offs2, out):
@@ -36,101 +39,104 @@ def tile_attend_gmp_ew_kernel(tc, dyT, hE, ew, w_words, w_scales, offs, offs2, o
         keep = ctx.enter_context(tc.tile_pool(name="keep", bufs=1))
         psum = ctx.enter_context(tc.psum_pool(name="psum", bufs=1))
 
-        def bank(i, shape):
-            return psum.tile(shape, F32, name="bank%d" % i, tag="bank%d" % i)
+        def in_psum(tag, shape):
+            return psum.tile(shape, F32, name=tag, tag=tag)
 
-        dst = keep.tile([P, E // 16], U16, name="dst")
-        src = keep.tile([P, E // 16], U16, name="src")
-        dy = [[keep.tile([P, V + SPARE], F32, name="dy%d%d" % (o, t)) for t in range(PACK)] for o in range(PASSES)]
-        h = [[keep.tile([P, PACK, HALF], F32, name="h%d%d" % (o, a)) for a in range(2)] for o in range(PASSES)]
+        dst = keep.tile([P, E // PER_COLUMN], U16, name="dst")
+        src = keep.tile([P, E // PER_COLUMN], U16, name="src")
+        dy = [[keep.tile([P, V + DY_SPARE], F32, name="dy%d%d" % (o, t)) for t in range(PACK)] for o in range(PASSES)]
+        h = [[keep.tile([P, PACK, HALF], F32, name="h%d%d" % (o, a)) for a in range(HALVES)] for o in range(PASSES)]
         ew_rows = keep.tile([P, P], F32, name="ew_rows")
         ew_cols = keep.tile([P, E // P], F32, name="ew_cols")
-        ew_wide = keep.tile([P, DIRECT_EDGES], F32, name="ew_wide")
+        ew_direct = keep.tile([P, DIRECT_EDGES], F32, name="ew_direct")
         w_codes = keep.tile([P, PASSES, D], U32, name="w_codes", align_bytes=64)
-        w_plane = keep.tile([P, PASSES * D], U8, name="w_plane", align_bytes=64)
+        w_scale = keep.tile([P, PASSES * D], U8, name="w_scale", align_bytes=64)
         ident = keep.tile([P, P], F32, name="ident")
-        codes = [[keep.tile([P, HALF], U32, name="codes%d%d" % (o, a), align_bytes=64) for a in range(2)] for o in range(PASSES)]
-        plane = [[keep.tile([P, HALF], U8, name="plane%d%d" % (o, a), align_bytes=64) for a in range(2)] for o in range(PASSES)]
-        dm = [keep.tile([P, E + (DM_SPARE if j < D_TILES - 1 else 0)], F32, name="dm%d" % j) for j in range(D_TILES)]
-
-        def dy_rows(o, t):
-            return dyT[o * K_PASS : (o + 1) * K_PASS, :].rearrange("(p t) v -> p t v", t=PACK)[:, t, :]
-
-        def h_rows(o, a):
-            return hE[o * K_PASS : (o + 1) * K_PASS, a * HALF : (a + 1) * HALF].rearrange("(p t) e -> p t e", t=PACK)
+        dz_codes = [
+            [keep.tile([P, HALF], U32, name="dz_codes%d%d" % (o, a), align_bytes=64) for a in range(HALVES)]
+            for o in range(PASSES)
+        ]
+        dz_scale = [
+            [keep.tile([P, HALF], U8, name="dz_scale%d%d" % (o, a), align_bytes=64) for a in range(HALVES)]
+            for o in range(PASSES)
+        ]
+        last_tile = D_TILES - 1
+        dm = [keep.tile([P, E + (DM_SPARE if j < last_tile else 0)], F32, name="dm%d" % j) for j in range(D_TILES)]
 
         make_identity(nc, ident[:])
-        nc.vector.memset(w_plane[:].bitcast(I32), 0)
+        nc.vector.memset(w_scale[:].bitcast(I32), 0)
         for o in range(PASSES):
             for t in range(PACK):
                 nc.vector.memset(dy[o][t][:, V:], 0.0)
-        for j in range(D_TILES - 1):
+        for j in range(last_tile):
             nc.vector.memset(dm[j][:, E:], 0.0)
 
-        nc.sync.dma_start(out=h[0][0][:, 0, :], in_=h_rows(0, 0)[:, 0, :])
+        def dy_plane(o, t):
+            return dyT[o * K_PASS : (o + 1) * K_PASS, :].rearrange("(p t) v -> p t v", t=PACK)[:, t, :]
+
+        def h_planes(o, a):
+            return hE[o * K_PASS : (o + 1) * K_PASS, a * HALF : (a + 1) * HALF].rearrange("(p t) e -> p t e", t=PACK)
+
+        nc.sync.dma_start(out=h[0][0][:, 0, :], in_=h_planes(0, 0)[:, 0, :])
         nc.sync.dma_start(dst[:], offs)
-        nc.sync.dma_start(out=dy[0][0][:, 0:V], in_=dy_rows(0, 0))
+        nc.sync.dma_start(out=dy[0][0][:, 0:V], in_=dy_plane(0, 0))
         for t in range(1, PACK):
-            nc.sync.dma_start(out=h[0][0][:, t, :], in_=h_rows(0, 0)[:, t, :])
-            nc.sync.dma_start(out=dy[0][t][:, 0:V], in_=dy_rows(0, t))
+            nc.sync.dma_start(out=h[0][0][:, t, :], in_=h_planes(0, 0)[:, t, :])
+            nc.sync.dma_start(out=dy[0][t][:, 0:V], in_=dy_plane(0, t))
         nc.sync.dma_start(out=ew_rows[:], in_=ew.rearrange("r (b c) -> (r b) c", c=P)[0:P, :])
         for t in range(0, PACK, 2):
-            nc.sync.dma_start(out=h[0][1][:, t : t + 2, :], in_=h_rows(0, 1)[:, t : t + 2, :])
-        nc.sync.dma_start(out=h[1][0][:], in_=h_rows(1, 0))
+            nc.sync.dma_start(out=h[0][1][:, t : t + 2, :], in_=h_planes(0, 1)[:, t : t + 2, :])
+        nc.sync.dma_start(out=h[1][0][:], in_=h_planes(1, 0))
         for t in range(PACK):
-            nc.sync.dma_start(out=dy[1][t][:, 0:V], in_=dy_rows(1, t))
-        nc.sync.dma_start(out=h[1][1][:], in_=h_rows(1, 1))
-        nc.sync.dma_start(out=ew_wide[:], in_=ew[:, E - DIRECT_EDGES : E])
+            nc.sync.dma_start(out=dy[1][t][:, 0:V], in_=dy_plane(1, t))
+        nc.sync.dma_start(out=h[1][1][:], in_=h_planes(1, 1))
+        nc.sync.dma_start(out=ew_direct[:], in_=ew[:, E - DIRECT_EDGES : E])
         nc.sync.dma_start(out=w_codes[:].bitcast(I32), in_=w_words.rearrange("o p d r -> p o (d r)").bitcast(I32))
-        for q in range(4):
+        for q in range(P // 32):
             nc.sync.dma_start(
-                out=w_plane[32 * q : 32 * q + 4, :].bitcast(I32).rearrange("f (o d) -> f o d", o=PASSES),
+                out=w_scale[32 * q : 32 * q + 4, :].bitcast(I32).rearrange("f (o d) -> f o d", o=PASSES),
                 in_=w_scales[:, 4 * q : 4 * q + 4, :].bitcast(I32).rearrange("o f d -> f o d"),
             )
         nc.sync.dma_start(src[:], offs2)
 
-        ew_bank = bank(7, [P, P])
-        nc.tensor.transpose(ew_bank[:], ew_rows[:], ident[:])
-        nc.vector.tensor_copy(out=ew_cols[:], in_=ew_bank[:, 0 : E // P])
+        ew_turned = in_psum("sum1", [P, P])
+        nc.tensor.transpose(ew_turned[:], ew_rows[:], ident[:])
+        nc.scalar.copy(out=ew_cols[:], in_=ew_turned[:, 0 : E // P])
 
-        def dst_cols(e0, n):
-            return dst[:, e0 // 16 : (e0 + n) // 16]
-
-        def h_piece(o, e0, n):
-            return h[o][e0 // HALF][:, :, e0 % HALF : e0 % HALF + n]
+        def targets(o, t, e0, n):
+            return dy[o][t][:].indirect(dst[:, e0 // PER_COLUMN : (e0 + n) // PER_COLUMN])
 
         def quantize(o, e0, n, woven):
-            cols = slice(e0 % HALF, e0 % HALF + n)
-            nc.vector.quantize_mx(
-                out=codes[o][e0 // HALF][:, cols].bitcast(E5M2X4), scales=plane[o][e0 // HALF][:, cols], in_=woven
-            )
+            a, cols = e0 // HALF, slice(e0 % HALF, e0 % HALF + n)
+            nc.vector.quantize_mx(out=dz_codes[o][a][:, cols].bitcast(E5M2X4), scales=dz_scale[o][a][:, cols], in_=woven)
 
-        turned = [(0, 0, HALF), (0, 1, HALF), (1, 0, HALF), (1, 1, HALF - DIRECT_EDGES)]
-        slope = [keep.tile([P, PACK, n], F32, name="slope%d" % i) for i, (o, a, n) in enumerate(turned)]
-        prod = [keep.tile([P, PACK, n], F32, name="prod%d" % i) for i, (o, a, n) in enumerate(turned)]
+        chunks = [(o, a, HALF) for o in range(PASSES) for a in range(HALVES)][:-1]
+        chunks.append((PASSES - 1, HALVES - 1, HALF - DIRECT_EDGES))
+        last_chunk = len(chunks) - 1
+        slope = [keep.tile([P, PACK, n], F32, name="slope%d" % i) for i, (o, a, n) in enumerate(chunks)]
+        prod = [keep.tile([P, PACK, n], F32, name="prod%d" % i) for i, (o, a, n) in enumerate(chunks)]
 
         def relu(i):
-            o, a, n = turned[i]
+            o, a, n = chunks[i]
             for t in range(PACK):
                 nc.scalar.activation(out=slope[i][:, t, :], in_=h[o][a][:, t, 0:n], func=ACT.Relu, scale=2.0)
 
         def gather_and_turn(i):
-            o, a, n = turned[i]
-            by_edge = psum.tile([P, n // P, PACK, P], F32, name="wide", tag="wide")
+            o, a, n = chunks[i]
+            by_edge = in_psum("by_edge", [P, n // P, PACK, P])
             for t in range(PACK):
-                nc.vector.tensor_tensor(prod[i][:, t, :], dy[o][t][:].indirect(dst_cols(a * HALF, n)), slope[i][:, t, :], ALU.mult)
+                nc.vector.tensor_tensor(prod[i][:, t, :], targets(o, t, a * HALF, n), slope[i][:, t, :], ALU.mult)
             order = [(b, t) for t in range(PACK) for b in range(n // P)]
-            for b, t in (sorted(order) if i >= 3 else order):
-                if True:
-                    nc.tensor.transpose(by_edge[:, b, t, :], prod[i][:, t, b * P : (b + 1) * P], ident[:])
+            for b, t in sorted(order) if i == last_chunk else order:
+                nc.tensor.transpose(by_edge[:, b, t, :], prod[i][:, t, b * P : (b + 1) * P], ident[:])
             return by_edge
 
         def weigh_and_weave(i, by_edge):
-            o, a, n = turned[i]
-            groups = [range(b0, min(b0 + 2, n // P)) for b0 in range(0, n // P, 2)]
-            rows = []
+            o, a, n = chunks[i]
+            groups = [range(b0, min(b0 + GROUP, n // P)) for b0 in range(0, n // P, GROUP)]
+            by_row = []
             for g, blocks in enumerate(groups):
-                by_row = bank(4 + g, [P, len(blocks), 2, P])
+                by_row.append(in_psum("by_row%d" % g, [P, len(blocks), 2, P]))
                 for b in blocks:
                     pairs = keep.tile([P, 2, P, 2], BF16, name="pairs%d%d" % (i, b))
                     col = a * (HALF // P) + b
@@ -142,80 +148,74 @@ def tile_attend_gmp_ew_kernel(tc, dyT, hE, ew, w_words, w_scales, offs, offs2, o
                     )
                     words = pairs[:].rearrange("e u p s -> e (u p s)").bitcast(F32)
                     for u in range(2):
-                        nc.tensor.transpose(by_row[:, b % 2, u, :], words[:, u * P : (u + 1) * P], ident[:])
-                rows.append(by_row)
+                        nc.tensor.transpose(by_row[g][:, b % GROUP, u, :], words[:, u * P : (u + 1) * P], ident[:])
             for g, blocks in enumerate(groups):
                 width = len(blocks) * P
-                woven = keep.tile([P, width * PACK], BF16, name="woven%d%d" % (i, g), tag="woven%d%d" % (i, g), align_bytes=64)
+                tag = "woven%d%d" % (i, g)
+                woven = keep.tile([P, width * PACK], BF16, name=tag, tag=tag, align_bytes=64)
                 nc.scalar.copy(
                     out=woven[:].bitcast(F32).rearrange("p (b e u) -> p b e u", b=len(blocks), u=2),
-                    in_=rows[g][:].rearrange("p b u e -> p b e u"),
+                    in_=by_row[g][:].rearrange("p b u e -> p b e u"),
                 )
-                quantize(o, a * HALF + g * UNIT, width, woven[:])
+                quantize(o, a * HALF + g * GROUP * P, width, woven[:])
 
         def direct():
-            o, n = PASSES - 1, DIRECT_EDGES
-            e0 = E - n
-            weighed = keep.tile([P, PACK, n], F32, name="weighed", tag="woven20", align_bytes=64)
+            o, a, n = PASSES - 1, HALVES - 1, DIRECT_EDGES
+            weighed = keep.tile([P, PACK, n], F32, name="weighed", tag="woven%d0" % (last_chunk - 1), align_bytes=64)
             rounded = keep.tile([P, PACK, n], BF16, name="rounded")
-            woven_direct = keep.tile([P, n, PACK], BF16, name="woven_direct", align_bytes=64)
+            woven = keep.tile([P, n, PACK], BF16, name="woven_direct", align_bytes=64)
             for t in range(PACK):
-                nc.vector.tensor_tensor(weighed[:, t, :], dy[o][t][:].indirect(dst_cols(e0, n)), ew_wide[:], ALU.mult)
-            for t0 in range(0, PACK, 2):
+                nc.vector.tensor_tensor(weighed[:, t, :], targets(o, t, E - n, n), ew_direct[:], ALU.mult)
+            for t in range(0, PACK, 2):
                 nc.vector.scalar_tensor_tensor(
-                    out=rounded[:, t0 : t0 + 2, :],
-                    in0=h_piece(o, e0, n)[:, t0 : t0 + 2, :],
+                    out=rounded[:, t : t + 2, :],
+                    in0=h[o][a][:, t : t + 2, HALF - n : HALF],
                     scalar=0.0,
-                    in1=weighed[:, t0 : t0 + 2, :],
+                    in1=weighed[:, t : t + 2, :],
                     op0=ALU.max,
                     op1=ALU.mult,
                 )
-            nc.vector.tensor_scalar_mul(woven_direct[:], rounded[:].rearrange("p t e -> p e t"), 2.0)
-            quantize(o, e0, n, woven_direct[:].rearrange("p e t -> p (e t)"))
-
-        def multiply(acc, j, o, a):
-            nc.tensor.matmul_mx(
-                out=acc,
-                lhsT=w_codes[:, o, j * P : (j + 1) * P].bitcast(E4M3X4),
-                lhsT_scale=w_plane[:, o * D + j * P : o * D + (j + 1) * P],
-                rhs=codes[o][a][:].bitcast(E5M2X4),
-                rhs_scale=plane[o][a][:],
-                start=(o == 0),
-                stop=(o == PASSES - 1),
-            )
+            nc.vector.tensor_scalar_mul(woven[:], rounded[:].rearrange("p t e -> p e t"), 2.0)
+            quantize(o, E - n, n, woven[:].rearrange("p e t -> p (e t)"))
 
         relu(0)
         by_edge = gather_and_turn(0)
-        for i in range(len(turned)):
-            if i == 0:
-                relu(1)
+        relu(1)
+        for i in range(len(chunks)):
             weigh_and_weave(i, by_edge)
-            if i + 2 < len(turned):
+            if i + 2 <= last_chunk:
                 relu(i + 2)
-            if i + 1 < len(turned):
+            if i + 1 <= last_chunk:
                 by_edge = gather_and_turn(i + 1)
         direct()
+
+        sum_tags = ("sum0", "sum1", "by_edge")
         for j in range(D_TILES):
-            accs = [bank(6 + a, [P, HALF])[:] for a in range(2)]
-            for a in range(2):
+            sums = [in_psum(sum_tags[(HALVES * j + a) % len(sum_tags)], [P, HALF]) for a in range(HALVES)]
+            for a in range(HALVES):
                 for o in range(PASSES):
-                    multiply(accs[a], j, o, a)
-            nc.scalar.copy(out=dm[j][:, 0:HALF], in_=accs[0])
+                    nc.tensor.matmul_mx(
+                        out=sums[a][:],
+                        lhsT=w_codes[:, o, j * P : (j + 1) * P].bitcast(E4M3X4),
+                        lhsT_scale=w_scale[:, o * D + j * P : o * D + (j + 1) * P],
+                        rhs=dz_codes[o][a][:].bitcast(E5M2X4),
+                        rhs_scale=dz_scale[o][a][:],
+                        start=(o == 0),
+                        stop=(o == PASSES - 1),
+                    )
+            nc.scalar.copy(out=dm[j][:, 0:HALF], in_=sums[0][:])
             if j == 0:
-                nc.vector.tensor_copy(out=dm[j][:, HALF:E], in_=accs[1])
+                nc.vector.tensor_copy(out=dm[j][:, HALF:E], in_=sums[1][:])
             else:
-                nc.scalar.copy(out=dm[j][:, HALF:E], in_=accs[1])
+                nc.scalar.copy(out=dm[j][:, HALF:E], in_=sums[1][:])
 
         for j in range(D_TILES):
-            looked = keep.tile([P, E], F32, name="looked%d" % j)
-            summed = keep.tile([P, V], F32, name="summed%d" % j)
-            cuts = (0, E) if j < D_TILES - 1 else (0, 512, 768, E)
+            cuts = LAST_CUTS if j == last_tile else (0, E)
             for c0, c1 in zip(cuts[:-1], cuts[1:]):
-                nc.vector.tensor_copy(looked[:, c0:c1], dm[j][:].indirect(src[:, c0 // 16 : c1 // 16]))
-                both = looked[:, c0:c1].rearrange("p (x k) -> p x k", k=K)
-                nodes = slice(c0 // K, c1 // K)
-                if j < D_TILES - 1:
-                    nc.gpsimd.tensor_tensor(summed[:, nodes], both[:, :, 0], both[:, :, 1], ALU.add)
-                else:
-                    nc.vector.tensor_tensor(summed[:, nodes], both[:, :, 0], both[:, :, 1], ALU.add)
-                nc.sync.dma_start(out=out[j * P : (j + 1) * P, nodes], in_=summed[:, nodes])
+                looked = keep.tile([P, c1 - c0], F32, name="looked%d_%d" % (j, c0))
+                summed = keep.tile([P, (c1 - c0) // K], F32, name="summed%d_%d" % (j, c0))
+                nc.vector.tensor_copy(looked[:], dm[j][:].indirect(src[:, c0 // PER_COLUMN : c1 // PER_COLUMN]))
+                both = looked[:].rearrange("p (x k) -> p x k", k=K)
+                adder = nc.vector if (j, c1) == (last_tile, E) else nc.gpsimd
+                adder.tensor_tensor(summed[:], both[:, :, 0], both[:, :, 1], ALU.add)
+                nc.sync.dma_start(out=out[j * P : (j + 1) * P, c0 // K : c1 // K], in_=summed[:])

from contextlib import ExitStack

import concourse.mybir as mybir
from concourse.masks import make_identity

V, K, E, D, DV = 512, 2, 1024, 512, 1024
FLOPS = 2 * DV * D * E

F32 = mybir.dt.float32
BF16 = mybir.dt.bfloat16
I32 = mybir.dt.int32
U32 = mybir.dt.uint32
U16 = mybir.dt.uint16
U8 = mybir.dt.uint8
E4M3X4 = mybir.dt.float8_e4m3fn_x4
E5M2X4 = mybir.dt.float8_e5m2_x4
ALU = mybir.AluOpType
ACT = mybir.ActivationFunctionType

P = 128
PACK = 4
K_PASS = P * PACK
PASSES = DV // K_PASS
HALF = 512
HALVES = E // HALF
D_TILES = D // P
PER_COLUMN = 16
GROUP = 2

DY_SPARE = 16
DM_SPARE = 352
DIRECT_EDGES = P
LAST_CUTS = (0, E // 2, 3 * E // 4, E)


def tile_attend_gmp_ew_kernel(tc, dyT, hE, ew, w_words, w_scales, offs, offs2, out):
    nc = tc.nc
    with ExitStack() as ctx:
        keep = ctx.enter_context(tc.tile_pool(name="keep", bufs=1))
        psum = ctx.enter_context(tc.psum_pool(name="psum", bufs=1))

        def in_psum(tag, shape):
            return psum.tile(shape, F32, name=tag, tag=tag)

        dst = keep.tile([P, E // PER_COLUMN], U16, name="dst")
        src = keep.tile([P, E // PER_COLUMN], U16, name="src")
        dy = [[keep.tile([P, V + DY_SPARE], F32, name="dy%d%d" % (o, t)) for t in range(PACK)] for o in range(PASSES)]
        h = [[keep.tile([P, PACK, HALF], F32, name="h%d%d" % (o, a)) for a in range(HALVES)] for o in range(PASSES)]
        ew_rows = keep.tile([P, P], F32, name="ew_rows")
        ew_cols = keep.tile([P, E // P], F32, name="ew_cols")
        ew_direct = keep.tile([P, DIRECT_EDGES], F32, name="ew_direct")
        w_codes = keep.tile([P, PASSES, D], U32, name="w_codes", align_bytes=64)
        w_scale = keep.tile([P, PASSES * D], U8, name="w_scale", align_bytes=64)
        ident = keep.tile([P, P], F32, name="ident")
        dz_codes = [
            [keep.tile([P, HALF], U32, name="dz_codes%d%d" % (o, a), align_bytes=64) for a in range(HALVES)]
            for o in range(PASSES)
        ]
        dz_scale = [
            [keep.tile([P, HALF], U8, name="dz_scale%d%d" % (o, a), align_bytes=64) for a in range(HALVES)]
            for o in range(PASSES)
        ]
        last_tile = D_TILES - 1
        dm = [keep.tile([P, E + (DM_SPARE if j < last_tile else 0)], F32, name="dm%d" % j) for j in range(D_TILES)]

        make_identity(nc, ident[:])
        nc.vector.memset(w_scale[:].bitcast(I32), 0)
        for o in range(PASSES):
            for t in range(PACK):
                nc.vector.memset(dy[o][t][:, V:], 0.0)
        for j in range(last_tile):
            nc.vector.memset(dm[j][:, E:], 0.0)

        def dy_plane(o, t):
            return dyT[o * K_PASS : (o + 1) * K_PASS, :].rearrange("(p t) v -> p t v", t=PACK)[:, t, :]

        def h_planes(o, a):
            return hE[o * K_PASS : (o + 1) * K_PASS, a * HALF : (a + 1) * HALF].rearrange("(p t) e -> p t e", t=PACK)

        nc.sync.dma_start(out=h[0][0][:, 0, :], in_=h_planes(0, 0)[:, 0, :])
        nc.sync.dma_start(dst[:], offs)
        nc.sync.dma_start(out=dy[0][0][:, 0:V], in_=dy_plane(0, 0))
        for t in range(1, PACK):
            nc.sync.dma_start(out=h[0][0][:, t, :], in_=h_planes(0, 0)[:, t, :])
            nc.sync.dma_start(out=dy[0][t][:, 0:V], in_=dy_plane(0, t))
        nc.sync.dma_start(out=ew_rows[:], in_=ew.rearrange("r (b c) -> (r b) c", c=P)[0:P, :])
        for t in range(0, PACK, 2):
            nc.sync.dma_start(out=h[0][1][:, t : t + 2, :], in_=h_planes(0, 1)[:, t : t + 2, :])
        nc.sync.dma_start(out=h[1][0][:], in_=h_planes(1, 0))
        for t in range(PACK):
            nc.sync.dma_start(out=dy[1][t][:, 0:V], in_=dy_plane(1, t))
        nc.sync.dma_start(out=h[1][1][:], in_=h_planes(1, 1))
        nc.sync.dma_start(out=ew_direct[:], in_=ew[:, E - DIRECT_EDGES : E])
        nc.sync.dma_start(out=w_codes[:].bitcast(I32), in_=w_words.rearrange("o p d r -> p o (d r)").bitcast(I32))
        for q in range(P // 32):
            nc.sync.dma_start(
                out=w_scale[32 * q : 32 * q + 4, :].bitcast(I32).rearrange("f (o d) -> f o d", o=PASSES),
                in_=w_scales[:, 4 * q : 4 * q + 4, :].bitcast(I32).rearrange("o f d -> f o d"),
            )
        nc.sync.dma_start(src[:], offs2)

        ew_turned = in_psum("sum1", [P, P])
        nc.tensor.transpose(ew_turned[:], ew_rows[:], ident[:])
        nc.scalar.copy(out=ew_cols[:], in_=ew_turned[:, 0 : E // P])

        def targets(o, t, e0, n):
            return dy[o][t][:].indirect(dst[:, e0 // PER_COLUMN : (e0 + n) // PER_COLUMN])

        def quantize(o, e0, n, woven):
            a, cols = e0 // HALF, slice(e0 % HALF, e0 % HALF + n)
            nc.vector.quantize_mx(out=dz_codes[o][a][:, cols].bitcast(E5M2X4), scales=dz_scale[o][a][:, cols], in_=woven)

        chunks = [(o, a, HALF) for o in range(PASSES) for a in range(HALVES)][:-1]
        chunks.append((PASSES - 1, HALVES - 1, HALF - DIRECT_EDGES))
        last_chunk = len(chunks) - 1
        slope = [keep.tile([P, PACK, n], F32, name="slope%d" % i) for i, (o, a, n) in enumerate(chunks)]
        prod = [keep.tile([P, PACK, n], F32, name="prod%d" % i) for i, (o, a, n) in enumerate(chunks)]

        def relu(i):
            o, a, n = chunks[i]
            for t in range(PACK):
                nc.scalar.activation(out=slope[i][:, t, :], in_=h[o][a][:, t, 0:n], func=ACT.Relu, scale=2.0)

        def gather_and_turn(i):
            o, a, n = chunks[i]
            by_edge = in_psum("by_edge", [P, n // P, PACK, P])
            for t in range(PACK):
                nc.vector.tensor_tensor(prod[i][:, t, :], targets(o, t, a * HALF, n), slope[i][:, t, :], ALU.mult)
            order = [(b, t) for t in range(PACK) for b in range(n // P)]
            for b, t in sorted(order) if i == last_chunk else order:
                nc.tensor.transpose(by_edge[:, b, t, :], prod[i][:, t, b * P : (b + 1) * P], ident[:])
            return by_edge

        def weigh_and_weave(i, by_edge):
            o, a, n = chunks[i]
            groups = [range(b0, min(b0 + GROUP, n // P)) for b0 in range(0, n // P, GROUP)]
            by_row = []
            for g, blocks in enumerate(groups):
                by_row.append(in_psum("by_row%d" % g, [P, len(blocks), 2, P]))
                for b in blocks:
                    pairs = keep.tile([P, 2, P, 2], BF16, name="pairs%d%d" % (i, b))
                    col = a * (HALF // P) + b
                    nc.scalar.activation(
                        out=pairs[:],
                        in_=by_edge[:, b].rearrange("e (u s) p -> e u p s", s=2),
                        func=ACT.Copy,
                        scale=ew_cols[:, col : col + 1],
                    )
                    words = pairs[:].rearrange("e u p s -> e (u p s)").bitcast(F32)
                    for u in range(2):
                        nc.tensor.transpose(by_row[g][:, b % GROUP, u, :], words[:, u * P : (u + 1) * P], ident[:])
            for g, blocks in enumerate(groups):
                width = len(blocks) * P
                tag = "woven%d%d" % (i, g)
                woven = keep.tile([P, width * PACK], BF16, name=tag, tag=tag, align_bytes=64)
                nc.scalar.copy(
                    out=woven[:].bitcast(F32).rearrange("p (b e u) -> p b e u", b=len(blocks), u=2),
                    in_=by_row[g][:].rearrange("p b u e -> p b e u"),
                )
                quantize(o, a * HALF + g * GROUP * P, width, woven[:])

        def direct():
            o, a, n = PASSES - 1, HALVES - 1, DIRECT_EDGES
            weighed = keep.tile([P, PACK, n], F32, name="weighed", tag="woven%d0" % (last_chunk - 1), align_bytes=64)
            rounded = keep.tile([P, PACK, n], BF16, name="rounded")
            woven = keep.tile([P, n, PACK], BF16, name="woven_direct", align_bytes=64)
            for t in range(PACK):
                nc.vector.tensor_tensor(weighed[:, t, :], targets(o, t, E - n, n), ew_direct[:], ALU.mult)
            for t in range(0, PACK, 2):
                nc.vector.scalar_tensor_tensor(
                    out=rounded[:, t : t + 2, :],
                    in0=h[o][a][:, t : t + 2, HALF - n : HALF],
                    scalar=0.0,
                    in1=weighed[:, t : t + 2, :],
                    op0=ALU.max,
                    op1=ALU.mult,
                )
            nc.vector.tensor_scalar_mul(woven[:], rounded[:].rearrange("p t e -> p e t"), 2.0)
            quantize(o, E - n, n, woven[:].rearrange("p e t -> p (e t)"))

        relu(0)
        by_edge = gather_and_turn(0)
        relu(1)
        for i in range(len(chunks)):
            weigh_and_weave(i, by_edge)
            if i + 2 <= last_chunk:
                relu(i + 2)
            if i + 1 <= last_chunk:
                by_edge = gather_and_turn(i + 1)
        direct()

        sum_tags = ("sum0", "sum1", "by_edge")
        for j in range(D_TILES):
            sums = [in_psum(sum_tags[(HALVES * j + a) % len(sum_tags)], [P, HALF]) for a in range(HALVES)]
            for a in range(HALVES):
                for o in range(PASSES):
                    nc.tensor.matmul_mx(
                        out=sums[a][:],
                        lhsT=w_codes[:, o, j * P : (j + 1) * P].bitcast(E4M3X4),
                        lhsT_scale=w_scale[:, o * D + j * P : o * D + (j + 1) * P],
                        rhs=dz_codes[o][a][:].bitcast(E5M2X4),
                        rhs_scale=dz_scale[o][a][:],
                        start=(o == 0),
                        stop=(o == PASSES - 1),
                    )
            nc.scalar.copy(out=dm[j][:, 0:HALF], in_=sums[0][:])
            if j == 0:
                nc.vector.tensor_copy(out=dm[j][:, HALF:E], in_=sums[1][:])
            else:
                nc.scalar.copy(out=dm[j][:, HALF:E], in_=sums[1][:])

        for j in range(D_TILES):
            cuts = LAST_CUTS if j == last_tile else (0, E)
            for c0, c1 in zip(cuts[:-1], cuts[1:]):
                looked = keep.tile([P, c1 - c0], F32, name="looked%d_%d" % (j, c0))
                summed = keep.tile([P, (c1 - c0) // K], F32, name="summed%d_%d" % (j, c0))
                nc.vector.tensor_copy(looked[:], dm[j][:].indirect(src[:, c0 // PER_COLUMN : c1 // PER_COLUMN]))
                both = looked[:].rearrange("p (x k) -> p x k", k=K)
                adder = nc.vector if (j, c1) == (last_tile, E) else nc.gpsimd
                adder.tensor_tensor(summed[:], both[:, :, 0], both[:, :, 1], ALU.add)
                nc.sync.dma_start(out=out[j * P : (j + 1) * P, c0 // K : c1 // K], in_=summed[:])
